import numpy as np
import ml_dtypes


def mxq(x, axis, fmt="e4m3"):
    dtype, down = {"e4m3": (ml_dtypes.float8_e4m3fn, 7), "e5m2": (ml_dtypes.float8_e5m2, 14)}[fmt]
    v = np.moveaxis(np.asarray(x, np.float32).astype(ml_dtypes.bfloat16).astype(np.float64), axis, -1)
    blocks = v.reshape(v.shape[:-1] + (-1, 32))
    amax = np.abs(blocks).max(-1, keepdims=True)
    byte = np.maximum(np.where(amax > 0, np.frexp(amax)[1] - 1 + 127, 0) - down, 1)
    scale = np.exp2(byte - 127.0)
    codes = (blocks / scale).astype(np.float32).astype(dtype).astype(np.float64)
    return np.moveaxis((codes * scale).reshape(v.shape), -1, axis)


WIDE = False


def mx_kscale(k):
    if not WIDE:
        return np.ones(k)
    levels = np.array([10, -10, 5, -5, 0])
    if k % 512:
        return np.exp2(np.random.permutation(np.resize(levels, k // 32))).repeat(32)
    a = np.empty((k // 512, 16))
    for p in range(k // 512):
        a[p, :8] = np.random.permutation(np.resize(levels, 8))
        for g in range(8):
            far = levels[np.abs(levels - a[p, g]) >= 10]
            a[p, g + 8] = far[np.random.randint(len(far))]
    return np.exp2(a.ravel()).repeat(32)


def f64(x):
    return np.asarray(x).astype(np.float64)


def striped8(idx):
    return np.asarray(idx).reshape(8, -1, 16).transpose(0, 2, 1).reshape(128, -1).astype(np.uint16)


def unstriped8(offs):
    return offs.reshape(8, 16, -1).transpose(0, 2, 1).reshape(8, -1).astype(np.int64)


def pick8(x, idx, run):
    r = np.arange(len(x))
    return x[r[:, None], idx[r % (8 * run) // run]]


E2M1 = np.array([0.0, 0.5, 1.0, 1.5, 2.0, 3.0, 4.0, 6.0, -0.0, -0.5, -1.0, -1.5, -2.0, -3.0, -4.0, -6.0])


def pack_weight(w, fmt):
    k, n = w.shape
    w = f64(np.asarray(w, np.float32).astype(ml_dtypes.bfloat16)).reshape(k // 32, 32, n)
    amax = np.abs(w).max(1)
    if fmt == "e4m3":
        byte = np.frexp(amax)[1] - 1 + 127 - 7
    else:
        mant, ex = np.frexp(amax / 6.0)
        byte = np.where(mant > 0.5, ex, ex - 1) + 127
    byte = np.clip(np.where(amax > 0, byte, 1), 1, 254)
    scaled = (w * np.exp2(127.0 - byte)[:, None, :]).reshape(k, n).astype(np.float32)
    by_word = np.ascontiguousarray(scaled.reshape(k // 512, 128, 4, n).transpose(0, 1, 3, 2))
    if fmt == "e4m3":
        words = by_word.astype(ml_dtypes.float8_e4m3fn).view(np.uint8)
    else:
        c = by_word.astype(ml_dtypes.float4_e2m1fn).view(np.uint8) & 0xF
        words = (c[..., 0::2] | (c[..., 1::2] << 4)).reshape(k // 512, 128, 2 * n)
    return np.ascontiguousarray(words), np.ascontiguousarray(byte.astype(np.uint8).reshape(k // 512, 16, n))


def unpack_weight(words, scales, fmt):
    g, _, n = scales.shape
    words = np.ascontiguousarray(words).reshape(g, 128, n, -1)
    if fmt == "e4m3":
        vals = words.view(ml_dtypes.float8_e4m3fn).astype(np.float64)
    else:
        nib = np.empty((g, 128, n, 4), np.uint8)
        nib[..., 0::2] = words & 0xF
        nib[..., 1::2] = words >> 4
        vals = E2M1[nib]
    vals = vals * np.repeat(np.exp2(scales.astype(np.float64) - 127.0), 8, axis=1)[..., None]
    return vals.transpose(0, 1, 3, 2).reshape(g * 512, n)


D, T, U, I, J, Q = 512, 1024, 1024, 512, 256, 128


def setup_inputs():
    n = np.random.standard_normal
    idx = np.stack([np.random.permutation(T)[:I] for _ in range(8)])
    idx2 = np.stack([np.random.permutation(U)[:I] for _ in range(8)])
    idx3 = np.stack([np.random.permutation(I)[:J] for _ in range(8)])
    idx4 = np.stack([np.random.permutation(T)[:J] for _ in range(8)])
    idx5 = np.stack([np.random.permutation(T)[:I] for _ in range(8)])
    fd = mx_kscale(D)
    keysp = pack_weight(n((D, T)) / fd[:, None], "e2m1")
    notesp = pack_weight(n((D, U)) / fd[:, None], "e4m3")
    return {
        "query": (n((D, Q)) * 1.0 / np.sqrt(D) * fd[:, None]).astype(np.float32),
        "keys_words": keysp[0],
        "keys_scales": keysp[1],
        "notes_words": notesp[0],
        "notes_scales": notesp[1],
        "offs": striped8(idx),
        "offs2": striped8(idx2),
        "offs3": striped8(idx3),
        "offs4": striped8(idx4),
        "offs5": striped8(idx5),
    }


def reference(query, keys_words, keys_scales, notes_words, notes_scales, offs, offs2, offs3, offs4, offs5):
    idx = unstriped8(offs)
    idx2 = unstriped8(offs2)
    idx3 = unstriped8(offs3)
    idx4 = unstriped8(offs4)
    idx5 = unstriped8(offs5)
    keysu = unpack_weight(keys_words, keys_scales, "e2m1")
    notesu = unpack_weight(notes_words, notes_scales, "e4m3")
    queryq = mxq(f64(query), 0, "e4m3")
    a = queryq.T @ keysu
    b = queryq.T @ notesu
    r = pick8(a, idx, 16) - pick8(b, idx2, 16)
    w = pick8(r, idx3, 16) * 2.0
    f1 = np.zeros((Q, T))
    f1[np.arange(Q)[:, None], idx4[np.arange(Q) % 128 // 16]] = w
    cc = a + f1
    y = pick8(cc, idx5, 16)
    return y

@@ -1,0 +1,124 @@
+from contextlib import ExitStack
+
+import concourse.mybir as mybir
+
+D, T, U, SLOTS, PICKS, Q = 512, 1024, 1024, 512, 256, 128
+FLOPS = 2 * D * Q * (T + U)
+
+F32 = mybir.dt.float32
+BF16 = mybir.dt.bfloat16
+I32 = mybir.dt.int32
+U32 = mybir.dt.uint32
+U16 = mybir.dt.uint16
+U8 = mybir.dt.uint8
+FP8X4 = mybir.dt.float8_e4m3fn_x4
+FP4X4 = mybir.dt.float4_e2m1fn_x4
+ADD = mybir.AluOpType.add
+SUBTRACT = mybir.AluOpType.subtract
+COPY = mybir.ActivationFunctionType.Copy
+
+P = 128
+PACK = 4
+GROUP = 16
+
+
+def tile_attend_secondpick_two_kernel(tc, query, keys_words, keys_scales, notes_words, notes_scales,
+                                       offs, offs2, offs3, offs4, offs5, out):
+    nc = tc.nc
+    with ExitStack() as ctx:
+        keep = ctx.enter_context(tc.tile_pool(name="keep", bufs=1))
+        psum = ctx.enter_context(tc.psum_pool(name="psum", bufs=1))
+
+        def load_scales(queue, plane, scales, quad):
+            queue.dma_start(out=plane[32 * quad : 32 * quad + 4, :].bitcast(I32),
+                            in_=scales[0].bitcast(I32)[4 * quad : 4 * quad + 4, :])
+
+        def load_list(name, src):
+            tile = keep.tile([P, src.shape[1]], U16, name=name)
+            nc.sync.dma_start(tile[:], src)
+            return tile
+
+        notes_plane = keep.tile([P, U], U8, align_bytes=64)
+        keys_plane = keep.tile([P, T], U8, align_bytes=64)
+        f1 = keep.tile([P, T], F32)
+        nc.vector.memset(notes_plane[:].bitcast(I32), 0)
+        nc.vector.memset(keys_plane[:].bitcast(I32), 0)
+        nc.vector.memset(f1[:], 0.0)
+
+        q_raw = keep.tile([P, PACK, Q], F32)
+        nc.sync.dma_start(out=q_raw[:], in_=query.rearrange("(p j) q -> p j q", j=PACK))
+        notes_flat = notes_words[0].rearrange("p n t -> p (n t)")
+        notes_lo = keep.tile([P, U // 2], U32, align_bytes=64)
+        notes_hi = keep.tile([P, U // 2], U32, align_bytes=64)
+        keys_codes = keep.tile([P, 2 * T], U8, align_bytes=64)
+        load_scales(nc.sync, notes_plane, notes_scales, 0)
+        load_scales(nc.sync, notes_plane, notes_scales, 1)
+        nc.sync.dma_start(out=notes_lo[:].bitcast(I32), in_=notes_flat[:, : 2 * U].bitcast(I32))
+        load_scales(nc.sync, notes_plane, notes_scales, 2)
+        load_scales(nc.sync, notes_plane, notes_scales, 3)
+        nc.sync.dma_start(out=notes_hi[:].bitcast(I32), in_=notes_flat[:, 2 * U :].bitcast(I32))
+        nc.sync.dma_start(out=keys_codes[:].bitcast(I32), in_=keys_words[0].bitcast(I32))
+        for quad in range(3):
+            load_scales(nc.sync, keys_plane, keys_scales, quad)
+        load_scales(nc.gpsimd, keys_plane, keys_scales, 3)
+        note_of_slot = load_list("note_of_slot", offs2)
+        token_of_slot = load_list("token_of_slot", offs)
+        slot_of_pick = load_list("slot_of_pick", offs3)
+        token_of_pick = load_list("token_of_pick", offs4)
+        token_of_out = load_list("token_of_out", offs5)
+
+        q_grouped = keep.tile([P, Q, PACK], BF16, align_bytes=64)
+        nc.vector.tensor_copy(out=q_grouped[:], in_=q_raw[:].rearrange("p j q -> p q j"))
+        q_codes = keep.tile([P, Q], U32, align_bytes=64)
+        q_plane = keep.tile([P, Q], U8, align_bytes=64)
+        nc.vector.quantize_mx(out=q_codes[:].bitcast(FP8X4), scales=q_plane[:],
+                              in_=q_grouped[:].rearrange("p q j -> p (q j)"))
+
+        def score(bank_name, codes, plane, lo, hi):
+            bank = psum.tile([P, hi - lo], F32, name=bank_name)
+            nc.tensor.matmul_mx(out=bank[:], lhsT=q_codes[:].bitcast(FP8X4), lhsT_scale=q_plane[:],
+                                rhs=codes, rhs_scale=plane[:, lo:hi], start=True, stop=True)
+            return bank
+
+        a = keep.tile([P, T], F32)
+        b = keep.tile([P, U], F32)
+        edges = [0, 256, 512, 768, 896, 1024]
+        pieces = list(zip(edges[:-1], edges[1:]))
+        for n, (lo, hi) in enumerate(pieces):
+            words = notes_lo[:, lo:hi] if hi <= U // 2 else notes_hi[:, lo - U // 2 : hi - U // 2]
+            bank = score(f"bank{n}", words.bitcast(FP8X4), notes_plane, lo, hi)
+            if n % 2 == 0:
+                nc.vector.tensor_copy(out=b[:, lo:hi], in_=bank[:])
+            else:
+                nc.scalar.activation(b[:, lo:hi], bank[:], COPY)
+
+        half = SLOTS // 2
+        cols = half // GROUP
+        b_listed = [keep.tile([P, half], F32, name=f"b_listed{h}") for h in range(2)]
+        for h in range(2):
+            nc.scalar.activation(b_listed[h][:], b[:].indirect(note_of_slot[:, h * cols : (h + 1) * cols]), COPY)
+
+        for n, (lo, hi) in enumerate(pieces):
+            bank = score(f"bank{(n + len(pieces)) % 8}", keys_codes[:, 2 * lo : 2 * hi].bitcast(FP4X4), keys_plane, lo, hi)
+            nc.vector.tensor_copy(out=a[:, lo:hi], in_=bank[:])
+
+        r = keep.tile([P, SLOTS], F32)
+        for h in range(2):
+            nc.vector.tensor_tensor(r[:, h * half : (h + 1) * half],
+                                    a[:].indirect(token_of_slot[:, h * cols : (h + 1) * cols]),
+                                    b_listed[h][:], SUBTRACT)
+
+        r_picked = keep.tile([P, PICKS], F32)
+        nc.vector.tensor_copy(r_picked[:, 0:128], r[:].indirect(slot_of_pick[:, 0:8]))
+        nc.scalar.activation(r_picked[:, 128:256], r[:].indirect(slot_of_pick[:, 8:16]), COPY)
+
+        nc.vector.tensor_tensor(f1[:].indirect(token_of_pick[:]), r_picked[:], r_picked[:], ADD)
+        cc = keep.tile([P, T], F32)
+        nc.vector.tensor_tensor(cc[:], a[:], f1[:], ADD)
+
+        out_lo = keep.tile([P, half], F32)
+        out_hi = keep.tile([P, half], F32)
+        nc.vector.tensor_copy(out_lo[:], cc[:].indirect(token_of_out[:, 0:cols]))
+        nc.scalar.activation(out_hi[:], cc[:].indirect(token_of_out[:, cols : 2 * cols]), COPY)
+        nc.sync.dma_start(out=out[:, 0:half], in_=out_lo[:])
+        nc.scalar.dma_start(out=out[:, half:SLOTS], in_=out_hi[:])

@@ -51,16 +51,14 @@ def tile_attend_secondpick_two_kernel(tc, query, keys_words, keys_scales, notes_
         notes_lo = keep.tile([P, U // 2], U32, align_bytes=64)
         notes_hi = keep.tile([P, U // 2], U32, align_bytes=64)
         keys_codes = keep.tile([P, 2 * T], U8, align_bytes=64)
-        load_scales(nc.sync, notes_plane, notes_scales, 0)
-        load_scales(nc.sync, notes_plane, notes_scales, 1)
+        for quad in range(3):
+            load_scales(nc.sync, notes_plane, notes_scales, quad)
         nc.sync.dma_start(out=notes_lo[:].bitcast(I32), in_=notes_flat[:, : 2 * U].bitcast(I32))
-        load_scales(nc.sync, notes_plane, notes_scales, 2)
         load_scales(nc.sync, notes_plane, notes_scales, 3)
         nc.sync.dma_start(out=notes_hi[:].bitcast(I32), in_=notes_flat[:, 2 * U :].bitcast(I32))
         nc.sync.dma_start(out=keys_codes[:].bitcast(I32), in_=keys_words[0].bitcast(I32))
-        for quad in range(3):
+        for quad in range(4):
             load_scales(nc.sync, keys_plane, keys_scales, quad)
-        load_scales(nc.gpsimd, keys_plane, keys_scales, 3)
         note_of_slot = load_list("note_of_slot", offs2)
         token_of_slot = load_list("token_of_slot", offs)
         slot_of_pick = load_list("slot_of_pick", offs3)

@@ -51,10 +51,9 @@ def tile_attend_secondpick_two_kernel(tc, query, keys_words, keys_scales, notes_
         notes_lo = keep.tile([P, U // 2], U32, align_bytes=64)
         notes_hi = keep.tile([P, U // 2], U32, align_bytes=64)
         keys_codes = keep.tile([P, 2 * T], U8, align_bytes=64)
-        for quad in range(3):
-            load_scales(nc.sync, notes_plane, notes_scales, quad)
+        for quad in range(4):
+            load_scales(nc.sync if quad < 2 else nc.scalar, notes_plane, notes_scales, quad)
         nc.sync.dma_start(out=notes_lo[:].bitcast(I32), in_=notes_flat[:, : 2 * U].bitcast(I32))
-        load_scales(nc.sync, notes_plane, notes_scales, 3)
         nc.sync.dma_start(out=notes_hi[:].bitcast(I32), in_=notes_flat[:, 2 * U :].bitcast(I32))
         nc.sync.dma_start(out=keys_codes[:].bitcast(I32), in_=keys_words[0].bitcast(I32))
         for quad in range(4):
@@ -96,15 +95,17 @@ def tile_attend_secondpick_two_kernel(tc, query, keys_words, keys_scales, notes_
         for h in range(2):
             nc.scalar.activation(b_listed[h][:], b[:].indirect(note_of_slot[:, h * cols : (h + 1) * cols]), COPY)
 
+        a_banks = []
         for n, (lo, hi) in enumerate(pieces):
             bank = score(f"bank{(n + len(pieces)) % 8}", keys_codes[:, 2 * lo : 2 * hi].bitcast(FP4X4), keys_plane, lo, hi)
             nc.vector.tensor_copy(out=a[:, lo:hi], in_=bank[:])
+            a_banks.append(bank)
 
         r = keep.tile([P, SLOTS], F32)
-        for h in range(2):
-            nc.vector.tensor_tensor(r[:, h * half : (h + 1) * half],
-                                    a[:].indirect(token_of_slot[:, h * cols : (h + 1) * cols]),
-                                    b_listed[h][:], SUBTRACT)
+        a_listed = keep.tile([P, half], F32)
+        nc.vector.tensor_tensor(r[:, 0:half], a[:].indirect(token_of_slot[:, 0:cols]), b_listed[0][:], SUBTRACT)
+        nc.scalar.activation(a_listed[:], a[:].indirect(token_of_slot[:, cols : 2 * cols]), COPY)
+        nc.vector.tensor_tensor(r[:, half:SLOTS], a_listed[:], b_listed[1][:], SUBTRACT)
 
         r_picked = keep.tile([P, PICKS], F32)
         nc.vector.tensor_copy(r_picked[:, 0:128], r[:].indirect(slot_of_pick[:, 0:8]))
@@ -112,7 +113,9 @@ def tile_attend_secondpick_two_kernel(tc, query, keys_words, keys_scales, notes_
 
         nc.vector.tensor_tensor(f1[:].indirect(token_of_pick[:]), r_picked[:], r_picked[:], ADD)
         cc = keep.tile([P, T], F32)
-        nc.vector.tensor_tensor(cc[:], a[:], f1[:], ADD)
+        for (lo, hi), bank in list(zip(pieces, a_banks))[:3]:
+            nc.vector.tensor_tensor(cc[:, lo:hi], f1[:, lo:hi], bank[:], ADD)
+        nc.gpsimd.tensor_tensor(cc[:, 768:T], f1[:, 768:T], a[:, 768:T], ADD)
 
         out_lo = keep.tile([P, half], F32)
         out_hi = keep.tile([P, half], F32)

@@ -14,6 +14,7 @@ U8 = mybir.dt.uint8
 FP8X4 = mybir.dt.float8_e4m3fn_x4
 FP4X4 = mybir.dt.float4_e2m1fn_x4
 ADD = mybir.AluOpType.add
+MULT = mybir.AluOpType.mult
 SUBTRACT = mybir.AluOpType.subtract
 COPY = mybir.ActivationFunctionType.Copy
 
@@ -29,8 +30,8 @@ def tile_attend_secondpick_two_kernel(tc, query, keys_words, keys_scales, notes_
         keep = ctx.enter_context(tc.tile_pool(name="keep", bufs=1))
         psum = ctx.enter_context(tc.psum_pool(name="psum", bufs=1))
 
-        def load_scales(queue, plane, scales, quad):
-            queue.dma_start(out=plane[32 * quad : 32 * quad + 4, :].bitcast(I32),
+        def load_scales(queue, plane, scales, quad, first=0):
+            queue.dma_start(out=plane[32 * quad + first : 32 * quad + first + 4, :].bitcast(I32),
                             in_=scales[0].bitcast(I32)[4 * quad : 4 * quad + 4, :])
 
         def load_list(name, src):
@@ -52,7 +53,7 @@ def tile_attend_secondpick_two_kernel(tc, query, keys_words, keys_scales, notes_
         notes_hi = keep.tile([P, U // 2], U32, align_bytes=64)
         keys_codes = keep.tile([P, 2 * T], U8, align_bytes=64)
         for quad in range(4):
-            load_scales(nc.sync if quad < 2 else nc.scalar, notes_plane, notes_scales, quad)
+            load_scales(nc.sync if quad < 2 else nc.scalar, notes_plane, notes_scales, quad, 4)
         nc.sync.dma_start(out=notes_lo[:].bitcast(I32), in_=notes_flat[:, : 2 * U].bitcast(I32))
         nc.sync.dma_start(out=notes_hi[:].bitcast(I32), in_=notes_flat[:, 2 * U :].bitcast(I32))
         nc.sync.dma_start(out=keys_codes[:].bitcast(I32), in_=keys_words[0].bitcast(I32))
@@ -83,7 +84,7 @@ def tile_attend_secondpick_two_kernel(tc, query, keys_words, keys_scales, notes_
         pieces = list(zip(edges[:-1], edges[1:]))
         for n, (lo, hi) in enumerate(pieces):
             words = notes_lo[:, lo:hi] if hi <= U // 2 else notes_hi[:, lo - U // 2 : hi - U // 2]
-            bank = score(f"bank{n}", words.bitcast(FP8X4), notes_plane, lo, hi)
+            bank = score(f"bank{n}", words.bitcast(FP8X4), notes_plane[4:P, :], lo, hi)
             if n % 2 == 0:
                 nc.vector.tensor_copy(out=b[:, lo:hi], in_=bank[:])
             else:
@@ -108,10 +109,10 @@ def tile_attend_secondpick_two_kernel(tc, query, keys_words, keys_scales, notes_
         nc.vector.tensor_tensor(r[:, half:SLOTS], a_listed[:], b_listed[1][:], SUBTRACT)
 
         r_picked = keep.tile([P, PICKS], F32)
-        nc.vector.tensor_copy(r_picked[:, 0:128], r[:].indirect(slot_of_pick[:, 0:8]))
-        nc.scalar.activation(r_picked[:, 128:256], r[:].indirect(slot_of_pick[:, 8:16]), COPY)
+        nc.vector.tensor_scalar(r_picked[:, 0:128], r[:].indirect(slot_of_pick[:, 0:8]), 2.0, 0.0, MULT, ADD)
+        nc.scalar.activation(r_picked[:, 128:256], r[:].indirect(slot_of_pick[:, 8:16]), COPY, scale=2.0)
 
-        nc.vector.tensor_tensor(f1[:].indirect(token_of_pick[:]), r_picked[:], r_picked[:], ADD)
+        nc.vector.tensor_copy(f1[:].indirect(token_of_pick[:]), r_picked[:])
         cc = keep.tile([P, T], F32)
         for (lo, hi), bank in list(zip(pieces, a_banks))[:3]:
             nc.vector.tensor_tensor(cc[:, lo:hi], f1[:, lo:hi], bank[:], ADD)

from contextlib import ExitStack

import concourse.mybir as mybir

D, T, U, SLOTS, PICKS, Q = 512, 1024, 1024, 512, 256, 128
FLOPS = 2 * D * Q * (T + U)

F32 = mybir.dt.float32
BF16 = mybir.dt.bfloat16
I32 = mybir.dt.int32
U32 = mybir.dt.uint32
U16 = mybir.dt.uint16
U8 = mybir.dt.uint8
FP8X4 = mybir.dt.float8_e4m3fn_x4
FP4X4 = mybir.dt.float4_e2m1fn_x4
ADD = mybir.AluOpType.add
MULT = mybir.AluOpType.mult
SUBTRACT = mybir.AluOpType.subtract
COPY = mybir.ActivationFunctionType.Copy

P = 128
PACK = 4
GROUP = 16


def tile_attend_secondpick_two_kernel(tc, query, keys_words, keys_scales, notes_words, notes_scales,
                                       offs, offs2, offs3, offs4, offs5, out):
    nc = tc.nc
    with ExitStack() as ctx:
        keep = ctx.enter_context(tc.tile_pool(name="keep", bufs=1))
        psum = ctx.enter_context(tc.psum_pool(name="psum", bufs=1))

        def load_scales(queue, plane, scales, quad, first=0):
            queue.dma_start(out=plane[32 * quad + first : 32 * quad + first + 4, :].bitcast(I32),
                            in_=scales[0].bitcast(I32)[4 * quad : 4 * quad + 4, :])

        def load_list(name, src):
            tile = keep.tile([P, src.shape[1]], U16, name=name)
            nc.sync.dma_start(tile[:], src)
            return tile

        notes_plane = keep.tile([P, U], U8, align_bytes=64)
        keys_plane = keep.tile([P, T], U8, align_bytes=64)
        f1 = keep.tile([P, T], F32)
        nc.vector.memset(notes_plane[:].bitcast(I32), 0)
        nc.vector.memset(keys_plane[:].bitcast(I32), 0)
        nc.vector.memset(f1[:], 0.0)

        q_raw = keep.tile([P, PACK, Q], F32)
        nc.sync.dma_start(out=q_raw[:], in_=query.rearrange("(p j) q -> p j q", j=PACK))
        notes_flat = notes_words[0].rearrange("p n t -> p (n t)")
        notes_lo = keep.tile([P, U // 2], U32, align_bytes=64)
        notes_hi = keep.tile([P, U // 2], U32, align_bytes=64)
        keys_codes = keep.tile([P, 2 * T], U8, align_bytes=64)
        for quad in range(4):
            load_scales(nc.sync if quad < 2 else nc.scalar, notes_plane, notes_scales, quad, 4)
        nc.sync.dma_start(out=notes_lo[:].bitcast(I32), in_=notes_flat[:, : 2 * U].bitcast(I32))
        nc.sync.dma_start(out=notes_hi[:].bitcast(I32), in_=notes_flat[:, 2 * U :].bitcast(I32))
        nc.sync.dma_start(out=keys_codes[:].bitcast(I32), in_=keys_words[0].bitcast(I32))
        for quad in range(4):
            load_scales(nc.sync, keys_plane, keys_scales, quad)
        note_of_slot = load_list("note_of_slot", offs2)
        token_of_slot = load_list("token_of_slot", offs)
        slot_of_pick = load_list("slot_of_pick", offs3)
        token_of_pick = load_list("token_of_pick", offs4)
        token_of_out = load_list("token_of_out", offs5)

        q_grouped = keep.tile([P, Q, PACK], BF16, align_bytes=64)
        nc.vector.tensor_copy(out=q_grouped[:], in_=q_raw[:].rearrange("p j q -> p q j"))
        q_codes = keep.tile([P, Q], U32, align_bytes=64)
        q_plane = keep.tile([P, Q], U8, align_bytes=64)
        nc.vector.quantize_mx(out=q_codes[:].bitcast(FP8X4), scales=q_plane[:],
                              in_=q_grouped[:].rearrange("p q j -> p (q j)"))

        def score(bank_name, codes, plane, lo, hi):
            bank = psum.tile([P, hi - lo], F32, name=bank_name)
            nc.tensor.matmul_mx(out=bank[:], lhsT=q_codes[:].bitcast(FP8X4), lhsT_scale=q_plane[:],
                                rhs=codes, rhs_scale=plane[:, lo:hi], start=True, stop=True)
            return bank

        a = keep.tile([P, T], F32)
        b = keep.tile([P, U], F32)
        edges = [0, 256, 512, 768, 896, 1024]
        pieces = list(zip(edges[:-1], edges[1:]))
        for n, (lo, hi) in enumerate(pieces):
            words = notes_lo[:, lo:hi] if hi <= U // 2 else notes_hi[:, lo - U // 2 : hi - U // 2]
            bank = score(f"bank{n}", words.bitcast(FP8X4), notes_plane[4:P, :], lo, hi)
            if n % 2 == 0:
                nc.vector.tensor_copy(out=b[:, lo:hi], in_=bank[:])
            else:
                nc.scalar.activation(b[:, lo:hi], bank[:], COPY)

        half = SLOTS // 2
        cols = half // GROUP
        b_listed = [keep.tile([P, half], F32, name=f"b_listed{h}") for h in range(2)]
        for h in range(2):
            nc.scalar.activation(b_listed[h][:], b[:].indirect(note_of_slot[:, h * cols : (h + 1) * cols]), COPY)

        a_banks = []
        for n, (lo, hi) in enumerate(pieces):
            bank = score(f"bank{(n + len(pieces)) % 8}", keys_codes[:, 2 * lo : 2 * hi].bitcast(FP4X4), keys_plane, lo, hi)
            nc.vector.tensor_copy(out=a[:, lo:hi], in_=bank[:])
            a_banks.append(bank)

        r = keep.tile([P, SLOTS], F32)
        a_listed = keep.tile([P, half], F32)
        nc.vector.tensor_tensor(r[:, 0:half], a[:].indirect(token_of_slot[:, 0:cols]), b_listed[0][:], SUBTRACT)
        nc.scalar.activation(a_listed[:], a[:].indirect(token_of_slot[:, cols : 2 * cols]), COPY)
        nc.vector.tensor_tensor(r[:, half:SLOTS], a_listed[:], b_listed[1][:], SUBTRACT)

        r_picked = keep.tile([P, PICKS], F32)
        nc.vector.tensor_scalar(r_picked[:, 0:128], r[:].indirect(slot_of_pick[:, 0:8]), 2.0, 0.0, MULT, ADD)
        nc.scalar.activation(r_picked[:, 128:256], r[:].indirect(slot_of_pick[:, 8:16]), COPY, scale=2.0)

        nc.vector.tensor_copy(f1[:].indirect(token_of_pick[:]), r_picked[:])
        cc = keep.tile([P, T], F32)
        for (lo, hi), bank in list(zip(pieces, a_banks))[:3]:
            nc.vector.tensor_tensor(cc[:, lo:hi], f1[:, lo:hi], bank[:], ADD)
        nc.gpsimd.tensor_tensor(cc[:, 768:T], f1[:, 768:T], a[:, 768:T], ADD)

        out_lo = keep.tile([P, half], F32)
        out_hi = keep.tile([P, half], F32)
        nc.vector.tensor_copy(out_lo[:], cc[:].indirect(token_of_out[:, 0:cols]))
        nc.scalar.activation(out_hi[:], cc[:].indirect(token_of_out[:, cols : 2 * cols]), COPY)
        nc.sync.dma_start(out=out[:, 0:half], in_=out_lo[:])
        nc.scalar.dma_start(out=out[:, half:SLOTS], in_=out_hi[:])
